import numpy as np
import ml_dtypes


def mxq(x, axis, fmt="e4m3"):
    dtype, down = {"e4m3": (ml_dtypes.float8_e4m3fn, 7), "e5m2": (ml_dtypes.float8_e5m2, 14)}[fmt]
    v = np.moveaxis(np.asarray(x, np.float32).astype(ml_dtypes.bfloat16).astype(np.float64), axis, -1)
    blocks = v.reshape(v.shape[:-1] + (-1, 32))
    amax = np.abs(blocks).max(-1, keepdims=True)
    byte = np.maximum(np.where(amax > 0, np.frexp(amax)[1] - 1 + 127, 0) - down, 1)
    scale = np.exp2(byte - 127.0)
    codes = (blocks / scale).astype(np.float32).astype(dtype).astype(np.float64)
    return np.moveaxis((codes * scale).reshape(v.shape), -1, axis)


WIDE = False


def mx_kscale(k):
    if not WIDE:
        return np.ones(k)
    levels = np.array([10, -10, 5, -5, 0])
    if k % 512:
        return np.exp2(np.random.permutation(np.resize(levels, k // 32))).repeat(32)
    a = np.empty((k // 512, 16))
    for p in range(k // 512):
        a[p, :8] = np.random.permutation(np.resize(levels, 8))
        for g in range(8):
            far = levels[np.abs(levels - a[p, g]) >= 10]
            a[p, g + 8] = far[np.random.randint(len(far))]
    return np.exp2(a.ravel()).repeat(32)


def f64(x):
    return np.asarray(x).astype(np.float64)


def striped(idx):
    return np.tile(idx.reshape(-1, 16).T, (8, 1)).astype(np.uint16)


def unstriped(offs):
    return offs[:16].T.reshape(-1).astype(np.int64)


E2M1 = np.array([0.0, 0.5, 1.0, 1.5, 2.0, 3.0, 4.0, 6.0, -0.0, -0.5, -1.0, -1.5, -2.0, -3.0, -4.0, -6.0])


def pack_weight(w, fmt):
    k, n = w.shape
    w = f64(np.asarray(w, np.float32).astype(ml_dtypes.bfloat16)).reshape(k // 32, 32, n)
    amax = np.abs(w).max(1)
    if fmt == "e4m3":
        byte = np.frexp(amax)[1] - 1 + 127 - 7
    else:
        mant, ex = np.frexp(amax / 6.0)
        byte = np.where(mant > 0.5, ex, ex - 1) + 127
    byte = np.clip(np.where(amax > 0, byte, 1), 1, 254)
    scaled = (w * np.exp2(127.0 - byte)[:, None, :]).reshape(k, n).astype(np.float32)
    by_word = np.ascontiguousarray(scaled.reshape(k // 512, 128, 4, n).transpose(0, 1, 3, 2))
    if fmt == "e4m3":
        words = by_word.astype(ml_dtypes.float8_e4m3fn).view(np.uint8)
    else:
        c = by_word.astype(ml_dtypes.float4_e2m1fn).view(np.uint8) & 0xF
        words = (c[..., 0::2] | (c[..., 1::2] << 4)).reshape(k // 512, 128, 2 * n)
    return np.ascontiguousarray(words), np.ascontiguousarray(byte.astype(np.uint8).reshape(k // 512, 16, n))


def unpack_weight(words, scales, fmt):
    g, _, n = scales.shape
    words = np.ascontiguousarray(words).reshape(g, 128, n, -1)
    if fmt == "e4m3":
        vals = words.view(ml_dtypes.float8_e4m3fn).astype(np.float64)
    else:
        nib = np.empty((g, 128, n, 4), np.uint8)
        nib[..., 0::2] = words & 0xF
        nib[..., 1::2] = words >> 4
        vals = E2M1[nib]
    vals = vals * np.repeat(np.exp2(scales.astype(np.float64) - 127.0), 8, axis=1)[..., None]
    return vals.transpose(0, 1, 3, 2).reshape(g * 512, n)


def gelu(v):
    return 0.5 * v * (1.0 + np.tanh(np.sqrt(2.0 / np.pi) * (v + 0.044715 * v**3)))


def twice(P):
    return np.random.permutation(np.repeat(np.arange(P), 2))


def bf(x):
    return np.asarray(x, np.float32).astype(ml_dtypes.bfloat16)


def planes(Y):
    n, m = Y.shape
    b = f64(bf(Y)).reshape(n // 32, 32, m)
    amax = np.abs(b).max(1)
    byte = np.clip(np.where(amax > 0, np.frexp(amax)[1] - 1 + 127 - 7, 1), 1, 254)
    codes = (b * np.exp2(127.0 - byte)[:, None, :]).reshape(n, m).astype(np.float32).astype(ml_dtypes.float8_e4m3fn).view(np.uint8)
    words = codes.reshape(n // 512, 128, 4, m).transpose(0, 1, 3, 2)
    return np.ascontiguousarray(words), np.ascontiguousarray(byte.astype(np.uint8).reshape(n // 512, 16, m))


K, T, H, S, P = 1024, 4096, 1024, 1024, 512

def setup_inputs():
    n = np.random.standard_normal
    s = mx_kscale(K)[:, None]
    u = mx_kscale(H)[:, None]
    d = {}
    d["tab_words"], d["tab_scales"] = pack_weight(n((K, T)) * s, "e4m3")
    d["offs"] = striped(np.random.permutation(T)[:S])
    d["pos1"] = striped(np.random.permutation(S)[:P])
    d["pos2"] = striped(np.random.permutation(S)[:P])
    d["pos3"] = striped(twice(P))
    d["w1"] = (n((K, H)) / s / K ** 0.5 * u.T).astype(np.float32)
    d["b1"] = (0.5 * n(H) * u[:, 0]).astype(np.float32)
    d["w4_words"], d["w4_scales"] = pack_weight(n((H, H)) / u / H ** 0.5, "e2m1")
    d["skip"] = (np.exp(0.3 * n(H)) / u[:, 0]).astype(np.float32)
    d["gain"] = np.exp(0.8 * n(H)).astype(np.float32)
    return d

def reference(tab_words, tab_scales, offs, pos1, pos2, pos3, w1, b1, w4_words, w4_scales, skip, gain):
    v = unpack_weight(tab_words, tab_scales, "e4m3")[:, unstriped(offs)]
    w4 = unpack_weight(w4_words, w4_scales, "e2m1")
    h = (mxq(f64(w1), 0, "e4m3").T @ v) + f64(b1)[:, None]
    h = np.maximum(h, 0.0)
    x = h[:, unstriped(pos1)] + h[:, unstriped(pos2)]
    joint = w4.T @ mxq(x, 0, "e4m3")
    raised = joint[:, unstriped(pos3)]
    y = f64(gain)[:, None] * np.tanh(raised + f64(skip)[:, None] * h)
    words, scales = planes(y)
    return y, words, scales

@@ -1,0 +1,287 @@
+from contextlib import ExitStack
+
+import concourse.mybir as mybir
+
+K, T, H, S, J = 1024, 4096, 1024, 1024, 512
+FLOPS = 2 * K * H * S + 2 * H * H * J
+
+F32 = mybir.dt.float32
+BF16 = mybir.dt.bfloat16
+I32 = mybir.dt.int32
+U32 = mybir.dt.uint32
+U16 = mybir.dt.uint16
+U8 = mybir.dt.uint8
+FP8X4 = mybir.dt.float8_e4m3fn_x4
+FP4X4 = mybir.dt.float4_e2m1fn_x4
+ACT = mybir.ActivationFunctionType
+ALU = mybir.AluOpType
+
+P = 128
+PACK = 4
+KP = P * PACK
+BANK = 512
+SPARE = 16
+KIB = 1024
+
+
+def tile_list_pipe_joint_encoder_kernel(
+    tc, tab_words, tab_scales, offs, pos1, pos2, pos3, w1, b1, w4_words, w4_scales, skip, gain, out_0, out_1, out_2
+):
+    nc = tc.nc
+    with ExitStack() as ctx:
+        keep = ctx.enter_context(tc.tile_pool(name="keep", bufs=1))
+        arena = ctx.enter_context(tc.tile_pool(name="arena", bufs=1))
+        ring = ctx.enter_context(tc.tile_pool(name="ring", bufs=2))
+        psum = ctx.enter_context(tc.psum_pool(name="psum", bufs=4))
+
+        def place(name, shape, dtype, kib):
+            return arena.tile(shape, dtype, name=name, offset=kib * KIB, align_bytes=64)
+
+        tab_s = keep.tile([P, T], U8, name="tab_s", align_bytes=64)
+        nc.vector.memset(tab_s[:].bitcast(I32), 0)
+        w4s_raw = keep.tile([P, 2, H], U8, name="w4s_raw", align_bytes=64)
+        nc.vector.memset(w4s_raw[:].bitcast(I32), 0)
+
+        def load_list(name, src):
+            lt = keep.tile([P, src.shape[1]], U16, name=name)
+            nc.sync.dma_start(lt[:], src)
+            return lt
+
+        def load_vector(name, vec):
+            vt = keep.tile([P, 2, PACK], F32, name=name)
+            nc.sync.dma_start(vt[:], vec.rearrange("(b p t) -> p b t", b=2, t=PACK))
+            return vt
+
+        def load_w1(a, b):
+            raw = place("w1_raw%d%d" % (a, b), [P, PACK, KP], F32, 32 + 8 * a)
+            nc.sync.dma_start(raw[:], w1[KP * a : KP * (a + 1), KP * b : KP * (b + 1)].rearrange("(p j) c -> p j c", j=PACK))
+            return raw
+
+        offs_t = load_list("offs_t", offs)
+        tab_w = []
+        for a in range(2):
+            tw = place("tab_w%d" % a, [P, T], U32, 16 * a)
+            nc.sync.dma_start(tw[:].bitcast(I32), tab_words[a].rearrange("p t i -> p (t i)").bitcast(I32))
+            tab_w.append(tw)
+        b1_t = load_vector("b1_t", b1)
+        pos1_t = load_list("pos1_t", pos1)
+        pos2_t = load_list("pos2_t", pos2)
+        w1_raw = {}
+        w1_raw[0, 0] = load_w1(0, 0)
+        w1_raw[1, 0] = load_w1(1, 0)
+        for q in range(4):
+            nc.gpsimd.dma_start(tab_s[32 * q : 32 * q + 8, :].bitcast(I32), tab_scales[:, 4 * q : 4 * q + 4, :].bitcast(I32))
+        for q in range(4):
+            nc.gpsimd.dma_start(
+                w4s_raw[32 * q : 32 * q + 4, :, :].bitcast(I32),
+                w4_scales[:, 4 * q : 4 * q + 4, :].rearrange("a r c -> r a c").bitcast(I32),
+            )
+        w4_raw = keep.tile([P, 2, 2 * H], U8, name="w4_raw", align_bytes=64)
+        nc.sync.dma_start(w4_raw[:].bitcast(I32), w4_words.rearrange("a p c -> p a c").bitcast(I32))
+        skip_t = load_vector("skip_t", skip)
+        pos3_t = load_list("pos3_t", pos3)
+        gain_t = load_vector("gain_t", gain)
+        joint = []
+        for n in range(8):
+            jt = keep.tile([P, J + SPARE], F32, name="joint%d" % n, align_bytes=64)
+            nc.vector.memset(jt[:, J:], 0.0)
+            joint.append(jt)
+
+        v_s = keep.tile([P, S], U8, name="v_s", align_bytes=64)
+        nc.vector.tensor_copy(v_s[:], tab_s[:].indirect(offs_t[:]))
+        v_w = []
+        for a in range(2):
+            vw = keep.tile([P, S], U32, name="v_w%d" % a, align_bytes=64)
+            nc.vector.tensor_copy(vw[:], tab_w[a][:].indirect(offs_t[:]))
+            v_w.append(vw)
+            if a == 0:
+                w4_s = place("w4_s", [P, 2 * H], U8, 0)
+                nc.vector.tensor_copy(
+                    w4_s[:].rearrange("p (u t m) -> p u t m", t=PACK, m=P),
+                    w4s_raw[:].rearrange("p a (g m t) -> p (a g) t m", t=PACK, m=P),
+                )
+
+        w1_q = {}
+        w1_s = {}
+
+        def cast_w1(a, b, half, engine_copy, bf):
+            src = w1_raw[a, b][:].rearrange("p j (m t) -> p m t j", t=PACK)[:, :, 2 * half : 2 * half + 2, :]
+            engine_copy(bf[:].rearrange("p t m j -> p m t j"), src)
+            return bf
+
+        def scalar_cast_w1(a, b, half):
+            bf = ring.tile([P, 2, P, PACK], BF16, name="w1_bf", tag="w1_bf", bufs=3, align_bytes=64)
+            return cast_w1(a, b, half, nc.scalar.copy, bf)
+
+        def quant_w1(a, b, half, bf):
+            q = keep.tile([P, 2 * P], U32, name="w1_q%d%d%d" % (a, b, half), align_bytes=64)
+            s = keep.tile([P, 2 * P], U8, name="w1_s%d%d%d" % (a, b, half), align_bytes=64)
+            nc.vector.quantize_mx(out=q[:].bitcast(FP8X4), scales=s[:], in_=bf[:].rearrange("p t m j -> p (t m j)"))
+            w1_q[a, b, half] = q
+            w1_s[a, b, half] = s
+
+        for a in range(2):
+            bf0 = cast_w1(a, 0, 0, nc.vector.tensor_copy, place("w1_bfv%d" % a, [P, 2, P, PACK], BF16, 16 + 2 * a))
+            bf1 = scalar_cast_w1(a, 0, 1)
+            quant_w1(a, 0, 0, bf0)
+            if a == 1:
+                w4_w = place("w4_w", [P, 2 * 2 * H], U8, 18)
+                nc.vector.tensor_copy(
+                    w4_w[:].bitcast(U16).rearrange("p (u t m) -> p u t m", t=PACK, m=P),
+                    w4_raw[:].bitcast(U16).rearrange("p a (g m t) -> p (a g) t m", t=PACK, m=P),
+                )
+            quant_w1(a, 0, 1, bf1)
+            w1_raw[a, 1] = load_w1(a, 1)
+
+        h = []
+
+        def first_stage(b, i):
+            ht = keep.tile([P, S], F32, name="h%d%d" % (b, i), align_bytes=64)
+            cols = slice(P * (i % 2), P * (i % 2 + 1))
+            for c in range(2):
+                acc = psum.tile([P, BANK], F32, name="acc1", tag="acc1")
+                js = slice(BANK * c, BANK * (c + 1))
+                for a in range(2):
+                    nc.tensor.matmul_mx(
+                        out=acc[:],
+                        lhsT=w1_q[a, b, i // 2][:, cols].bitcast(FP8X4),
+                        lhsT_scale=w1_s[a, b, i // 2][:, cols],
+                        rhs=v_w[a][:, js].bitcast(FP8X4),
+                        rhs_scale=v_s[4 * a : P, js],
+                        start=(a == 0),
+                        stop=(a == 1),
+                    )
+                if (b, i, c) == (0, 0, 1):
+                    nc.vector.tensor_scalar(ht[:, js], acc[:], b1_t[:, b, i : i + 1], 0.0, ALU.add, ALU.max)
+                else:
+                    nc.scalar.activation(ht[:, js], acc[:], ACT.Relu, bias=b1_t[:, b, i : i + 1])
+            h.append(ht)
+
+        x_f = {}
+        x_q = []
+        x_s = []
+        picked = {}
+
+        def pick_first(n):
+            g = ring.tile([P, J], F32, name="picked", tag="picked", align_bytes=64)
+            nc.vector.tensor_copy(g[:], h[n][:].indirect(pos1_t[:]))
+            picked[n] = g
+
+        def pick_second(n):
+            b, i = divmod(n, PACK)
+            if i == 0:
+                x_f[b] = place("x_f%d" % b, [P, PACK, J], F32, 48 + 8 * b)
+            nc.vector.tensor_tensor(x_f[b][:, i, :], h[n][:].indirect(pos2_t[:]), picked[n][:], ALU.add)
+
+        def interleave(engine_copy, dst, src):
+            engine_copy(
+                dst.rearrange("p (c i) t -> p c t i", i=PACK),
+                src.rearrange("p t (c i) -> p c t i", i=PACK),
+            )
+
+        def quant_x(b, engine_copy):
+            bf = ring.tile([P, J, PACK], BF16, name="x_bf", tag="bf4k", bufs=3, align_bytes=64)
+            interleave(engine_copy, bf[:], x_f[b][:])
+            q = keep.tile([P, J], U32, name="x_q%d" % b, align_bytes=64)
+            s = keep.tile([P, J], U8, name="x_s%d" % b, align_bytes=64)
+            nc.vector.quantize_mx(out=q[:].bitcast(FP8X4), scales=s[:], in_=bf[:].rearrange("p c t -> p (c t)"))
+            x_q.append(q)
+            x_s.append(s)
+
+        sh_at = [4, 8, 12, 22, 56, 60, 26, 64]
+        sh = {}
+
+        def scale_h(n, engine):
+            st = place("sh%d" % n, [P, S], F32, sh_at[n])
+            factor = skip_t[:, n // PACK, n % PACK : n % PACK + 1]
+            if engine == "scalar":
+                nc.scalar.activation(st[:], h[n][:], ACT.Copy, scale=factor)
+            elif engine == "vector":
+                nc.vector.tensor_scalar(st[:], h[n][:], factor, None, ALU.mult)
+            else:
+                nc.gpsimd.tensor_scalar(st[:], h[n][:], factor, 0.0, ALU.mult, ALU.add)
+            sh[n] = st
+
+        late = {1: [(0, 1, 0)], 2: [(1, 1, 0), (0, 1, 1)], 3: [(1, 1, 1)]}
+        for n in range(8):
+            first_stage(*divmod(n, PACK))
+            pick_first(n)
+            if n > 0:
+                pick_second(n - 1)
+            for a, b, half in late.get(n, []):
+                quant_w1(a, b, half, scalar_cast_w1(a, b, half))
+            if n == 7:
+                quant_x(0, nc.scalar.copy)
+        pick_second(7)
+        quant_x(1, nc.vector.tensor_copy)
+        for n in range(PACK):
+            scale_h(n, "scalar")
+
+        def second_pass(acc, g, t, a):
+            u = (2 * a + g) * PACK + t
+            nc.tensor.matmul_mx(
+                out=acc[:],
+                lhsT=w4_w[:, 2 * P * u : 2 * P * (u + 1)].bitcast(FP4X4),
+                lhsT_scale=w4_s[:, P * u : P * (u + 1)],
+                rhs=x_q[a][:].bitcast(FP8X4),
+                rhs_scale=x_s[a][:],
+                start=(a == 0),
+                stop=(a == 1),
+            )
+
+        def second_stage(g):
+            accs = [psum.tile([P, BANK], F32, name="acc2", tag="acc2") for t in range(PACK)]
+            for a in range(2):
+                for t in range(PACK):
+                    second_pass(accs[t], g, t, a)
+            for t in range(PACK):
+                nc.scalar.copy(joint[PACK * g + t][:, 0:J], accs[t][:])
+
+        second_stage(0)
+        for n in (4, 5):
+            scale_h(n, "vector")
+
+        y_s = [keep.tile([P, S], U8, name="y_s%d" % g, align_bytes=64) for g in range(2)]
+
+        def finish(g, c0, c1, y):
+            w = c1 - c0
+            bf = ring.tile([P, w, PACK], BF16, name="y_bf", tag="bf4k", bufs=3, align_bytes=64)
+            interleave(nc.vector.tensor_copy, bf[:], y[:])
+            q = ring.tile([P, w], U32, name="y_q", tag="y_q", bufs=3, align_bytes=64)
+            nc.vector.quantize_mx(out=q[:].bitcast(FP8X4), scales=y_s[g][:, c0:c1], in_=bf[:].rearrange("p c t -> p (c t)"))
+            nc.sync.dma_start(out_1[g].rearrange("p m t -> p (m t)")[:, PACK * c0 : PACK * c1].bitcast(I32), q[:].bitcast(I32))
+            if c1 == S:
+                for q4 in range(4):
+                    eng = nc.sync if q4 % 2 == 0 or g == 0 else nc.scalar
+                    eng.dma_start(out_2[g, 4 * q4 : 4 * q4 + 4, :].bitcast(I32), y_s[g][32 * q4 : 32 * q4 + 4, :].bitcast(I32))
+
+        chunks = [(0, 0, 512, 32), (0, 512, 1024, 40), (1, 0, 512, 48), (1, 512, 768, 32), (1, 768, 1024, 36)]
+        waiting = None
+        for k, (g, c0, c1, y_at) in enumerate(chunks):
+            w = c1 - c0
+            last = k == len(chunks) - 1
+            y = place("y%d" % k, [P, PACK, w], F32, y_at)
+            rows = out_0[KP * g : KP * (g + 1), c0:c1].rearrange("(p t) j -> p t j", t=PACK)
+            for t in range(PACK):
+                n = PACK * g + t
+                z = ring.tile([P, w], F32, name="z", tag="z", bufs=4, align_bytes=64)
+                nc.vector.tensor_tensor(z[:], joint[n][:].indirect(pos3_t[:, c0 // 16 : c1 // 16]), sh[n][:, c0:c1], ALU.add)
+                th = ring.tile([P, w], F32, name="th", tag="th", bufs=2, align_bytes=64)
+                nc.scalar.activation(th[:], z[:], ACT.Tanh)
+                factor = gain_t[:, g, t : t + 1]
+                if last and t == PACK - 1:
+                    nc.vector.tensor_scalar(y[:, t, :], th[:], factor, None, ALU.mult)
+                else:
+                    nc.scalar.activation(y[:, t, :], th[:], ACT.Copy, scale=factor)
+                if t == 1 and waiting is not None:
+                    finish(*waiting)
+                if last and t % 2 == 1:
+                    nc.sync.dma_start(rows[:, t - 1 : t + 1, :], y[:, t - 1 : t + 1, :])
+            if not last:
+                nc.sync.dma_start(rows, y[:])
+            waiting = (g, c0, c1, y)
+            if k == 0:
+                second_stage(1)
+                for n in (6, 7):
+                    scale_h(n, "scalar")
+        finish(*waiting)

@@ -20,8 +20,31 @@ P = 128
 PACK = 4
 KP = P * PACK
 BANK = 512
+SLICES = H // P
+QUADRANTS = 4
+PER_COLUMN = 16
 SPARE = 16
+HALF_J = J // 2
 KIB = 1024
+
+TAB_W_AT = [0, 16]
+W1_RAW_AT = [32, 40]
+TAB_S_AT = 40
+W4S_ROWS_AT = 47.5
+V_S_AT = [49, 48]
+W4_RAW_AT = [0, 2]
+W1_BF_VECTOR_AT = 16
+W1_BF_SCALAR_AT = 68
+W4_W_AT = [17, 0]
+W4_S_AT = 14.5
+W1_Q_LATE_AT = 85.5
+PICKED_AT = {3: 78, 4: 80, 5: 82}
+X_F_AT = [98, 56]
+X_BF_AT = [84, 88]
+X_Q_AT = [96, 92]
+SH_AT = [40, 44, 32, 36, 60, 88, 56, 64]
+CHUNKS = [(0, 0, 512, 4), (0, 512, 1024, 23), (1, 0, 512, 98), (1, 512, 768, 4), (1, 768, 1024, 8)]
+LATE_WEIGHTS = {2: [(0, 1, 0), (1, 1, 0)], 3: [(0, 1, 1)], 4: [(1, 1, 1)]}
 
 
 def tile_list_pipe_joint_encoder_kernel(
@@ -35,253 +58,294 @@ def tile_list_pipe_joint_encoder_kernel(
         psum = ctx.enter_context(tc.psum_pool(name="psum", bufs=4))
 
         def place(name, shape, dtype, kib):
-            return arena.tile(shape, dtype, name=name, offset=kib * KIB, align_bytes=64)
+            return arena.tile(shape, dtype, name=name, offset=int(kib * KIB), align_bytes=64)
 
-        tab_s = keep.tile([P, T], U8, name="tab_s", align_bytes=64)
-        nc.vector.memset(tab_s[:].bitcast(I32), 0)
-        w4s_raw = keep.tile([P, 2, H], U8, name="w4s_raw", align_bytes=64)
-        nc.vector.memset(w4s_raw[:].bitcast(I32), 0)
+        def entries(list_tile, first, end):
+            return list_tile[:, first // PER_COLUMN : end // PER_COLUMN]
+
+        def load_scale_rows(name, src, kib):
+            rows = place(name, [P, src.shape[2] // 4], I32, kib)
+            nc.sync.dma_start(rows[0:32, :], src.rearrange("a q c -> (a q) c").bitcast(I32))
+            nc.vector.memset(rows[32:64, :], 0)
+            nc.vector.memset(rows[64:P, :], 0)
+            return rows
+
+        def move_to_plane(plane, rows, a):
+            for quadrant in range(QUADRANTS):
+                first = 16 * a + 4 * quadrant
+                nc.sync.dma_start(plane[32 * quadrant : 32 * quadrant + 4, :].bitcast(I32), rows[first : first + 4, :].bitcast(I32))
 
         def load_list(name, src):
-            lt = keep.tile([P, src.shape[1]], U16, name=name)
-            nc.sync.dma_start(lt[:], src)
-            return lt
+            list_tile = keep.tile([P, src.shape[1]], U16, name=name)
+            nc.sync.dma_start(list_tile[:], src)
+            return list_tile
 
         def load_vector(name, vec):
-            vt = keep.tile([P, 2, PACK], F32, name=name)
-            nc.sync.dma_start(vt[:], vec.rearrange("(b p t) -> p b t", b=2, t=PACK))
-            return vt
+            values = keep.tile([P, 2, PACK], F32, name=name)
+            nc.gpsimd.dma_start(values[:], vec.rearrange("(b p t) -> p b t", b=2, t=PACK))
+            return values
 
         def load_w1(a, b):
-            raw = place("w1_raw%d%d" % (a, b), [P, PACK, KP], F32, 32 + 8 * a)
+            raw = place("w1_raw%d%d" % (a, b), [P, PACK, KP], F32, W1_RAW_AT[a])
             nc.sync.dma_start(raw[:], w1[KP * a : KP * (a + 1), KP * b : KP * (b + 1)].rearrange("(p j) c -> p j c", j=PACK))
             return raw
 
+        def load_table(a):
+            words = place("tab_w%d" % a, [P, T], U32, TAB_W_AT[a])
+            nc.sync.dma_start(words[:].bitcast(I32), tab_words[a].rearrange("p t i -> p (t i)").bitcast(I32))
+            return words
+
+        def load_w4(b):
+            raw = place("w4_raw%d" % b, [P, 2, 2 * KP], U8, W4_RAW_AT[b])
+            src = w4_words.rearrange("a p c -> p a c")[:, :, 2 * KP * b : 2 * KP * (b + 1)]
+            nc.sync.dma_start(raw[:].bitcast(I32), src.bitcast(I32))
+            return raw
+
         offs_t = load_list("offs_t", offs)
-        tab_w = []
-        for a in range(2):
-            tw = place("tab_w%d" % a, [P, T], U32, 16 * a)
-            nc.sync.dma_start(tw[:].bitcast(I32), tab_words[a].rearrange("p t i -> p (t i)").bitcast(I32))
-            tab_w.append(tw)
-        b1_t = load_vector("b1_t", b1)
+        tab_s = load_scale_rows("tab_s", tab_scales, TAB_S_AT)
+        w4s_rows = load_scale_rows("w4s_rows", w4_scales, W4S_ROWS_AT)
+        tab_w = [load_table(0)]
         pos1_t = load_list("pos1_t", pos1)
         pos2_t = load_list("pos2_t", pos2)
-        w1_raw = {}
-        w1_raw[0, 0] = load_w1(0, 0)
-        w1_raw[1, 0] = load_w1(1, 0)
-        for q in range(4):
-            nc.gpsimd.dma_start(tab_s[32 * q : 32 * q + 8, :].bitcast(I32), tab_scales[:, 4 * q : 4 * q + 4, :].bitcast(I32))
-        for q in range(4):
-            nc.gpsimd.dma_start(
-                w4s_raw[32 * q : 32 * q + 4, :, :].bitcast(I32),
-                w4_scales[:, 4 * q : 4 * q + 4, :].rearrange("a r c -> r a c").bitcast(I32),
-            )
-        w4_raw = keep.tile([P, 2, 2 * H], U8, name="w4_raw", align_bytes=64)
-        nc.sync.dma_start(w4_raw[:].bitcast(I32), w4_words.rearrange("a p c -> p a c").bitcast(I32))
-        skip_t = load_vector("skip_t", skip)
         pos3_t = load_list("pos3_t", pos3)
-        gain_t = load_vector("gain_t", gain)
-        joint = []
-        for n in range(8):
-            jt = keep.tile([P, J + SPARE], F32, name="joint%d" % n, align_bytes=64)
-            nc.vector.memset(jt[:, J:], 0.0)
-            joint.append(jt)
+        tab_w.append(load_table(1))
+        w1_raw = {(0, 0): load_w1(0, 0)}
 
-        v_s = keep.tile([P, S], U8, name="v_s", align_bytes=64)
-        nc.vector.tensor_copy(v_s[:], tab_s[:].indirect(offs_t[:]))
+        vs_rows = keep.tile([P, S], U8, name="vs_rows", align_bytes=64)
+        nc.vector.tensor_copy(vs_rows[:], tab_s[:].bitcast(U8).indirect(offs_t[:]))
+        w4s_dealt = keep.tile([P, H], U8, name="w4s_dealt", align_bytes=64)
+        nc.vector.tensor_copy(
+            w4s_dealt[:].rearrange("p (b t m) -> p b t m", t=PACK, m=P),
+            w4s_rows[:].bitcast(U8).rearrange("p (b m t) -> p b t m", t=PACK, m=P),
+        )
+
+        def table_plane(a):
+            plane = place("v_s%d" % a, [P, S], U8, V_S_AT[a])
+            nc.gpsimd.memset(plane[:].bitcast(I32), 0)
+            move_to_plane(plane, vs_rows, a)
+            return plane
+
+        v_s = [table_plane(0)]
+        b1_t = load_vector("b1_t", b1)
+        skip_t = load_vector("skip_t", skip)
+        gain_t = load_vector("gain_t", gain)
+        w1_raw[1, 0] = load_w1(1, 0)
+        v_s.append(table_plane(1))
+
+        joint = []
+        for n in range(SLICES):
+            joint_n = keep.tile([P, J + SPARE], F32, name="joint%d" % n, align_bytes=64)
+            nc.gpsimd.memset(joint_n[:, J:], 0.0)
+            joint.append(joint_n)
+
         v_w = []
         for a in range(2):
-            vw = keep.tile([P, S], U32, name="v_w%d" % a, align_bytes=64)
-            nc.vector.tensor_copy(vw[:], tab_w[a][:].indirect(offs_t[:]))
-            v_w.append(vw)
+            words = keep.tile([P, S], U32, name="v_w%d" % a, align_bytes=64)
+            nc.vector.tensor_copy(words[:], tab_w[a][:].indirect(offs_t[:]))
+            v_w.append(words)
             if a == 0:
-                w4_s = place("w4_s", [P, 2 * H], U8, 0)
-                nc.vector.tensor_copy(
-                    w4_s[:].rearrange("p (u t m) -> p u t m", t=PACK, m=P),
-                    w4s_raw[:].rearrange("p a (g m t) -> p (a g) t m", t=PACK, m=P),
-                )
+                w4_raw = [load_w4(0), load_w4(1)]
 
         w1_q = {}
         w1_s = {}
+        w4_w = {}
 
-        def cast_w1(a, b, half, engine_copy, bf):
-            src = w1_raw[a, b][:].rearrange("p j (m t) -> p m t j", t=PACK)[:, :, 2 * half : 2 * half + 2, :]
-            engine_copy(bf[:].rearrange("p t m j -> p m t j"), src)
-            return bf
+        def round_w1(a, b, pair, copy, rounded):
+            src = w1_raw[a, b][:].rearrange("p j (m t) -> p m j t", t=PACK)[:, :, :, 2 * pair : 2 * pair + 2]
+            copy(rounded[:].rearrange("p t m j -> p m j t"), src)
+            return rounded
 
-        def scalar_cast_w1(a, b, half):
-            bf = ring.tile([P, 2, P, PACK], BF16, name="w1_bf", tag="w1_bf", bufs=3, align_bytes=64)
-            return cast_w1(a, b, half, nc.scalar.copy, bf)
+        def round_w1_on_scalar(a, b, pair):
+            kib = W1_BF_SCALAR_AT + 2 * (4 * b + 2 * pair + a)
+            return round_w1(a, b, pair, nc.scalar.copy, place("w1_bf%d%d%d" % (a, b, pair), [P, 2, P, PACK], BF16, kib))
 
-        def quant_w1(a, b, half, bf):
-            q = keep.tile([P, 2 * P], U32, name="w1_q%d%d%d" % (a, b, half), align_bytes=64)
-            s = keep.tile([P, 2 * P], U8, name="w1_s%d%d%d" % (a, b, half), align_bytes=64)
-            nc.vector.quantize_mx(out=q[:].bitcast(FP8X4), scales=s[:], in_=bf[:].rearrange("p t m j -> p (t m j)"))
-            w1_q[a, b, half] = q
-            w1_s[a, b, half] = s
+        def quantise_w1(a, b, pair, rounded):
+            if (a, b, pair) == (1, 1, 0):
+                codes = place("w1_q110", [P, 2 * P], U32, W1_Q_LATE_AT)
+            else:
+                codes = keep.tile([P, 2 * P], U32, name="w1_q%d%d%d" % (a, b, pair), align_bytes=64)
+            plane = keep.tile([P, 2 * P], U8, name="w1_s%d%d%d" % (a, b, pair), align_bytes=64)
+            nc.vector.quantize_mx(out=codes[:].bitcast(FP8X4), scales=plane[:], in_=rounded[:].rearrange("p t m j -> p (t m j)"))
+            w1_q[a, b, pair] = codes
+            w1_s[a, b, pair] = plane
+
+        def deal_w4(b):
+            w4_w[b] = place("w4_w%d" % b, [P, 2 * 2 * KP], U8, W4_W_AT[b])
+            nc.vector.tensor_copy(
+                w4_w[b][:].bitcast(U16).rearrange("p (a t m) -> p a t m", t=PACK, m=P),
+                w4_raw[b][:].bitcast(U16).rearrange("p a (m t) -> p a t m", t=PACK),
+            )
 
         for a in range(2):
-            bf0 = cast_w1(a, 0, 0, nc.vector.tensor_copy, place("w1_bfv%d" % a, [P, 2, P, PACK], BF16, 16 + 2 * a))
-            bf1 = scalar_cast_w1(a, 0, 1)
-            quant_w1(a, 0, 0, bf0)
+            first_pair = round_w1(a, 0, 0, nc.vector.tensor_copy, place("w1_bfv%d" % a, [P, 2, P, PACK], BF16, W1_BF_VECTOR_AT))
+            second_pair = round_w1_on_scalar(a, 0, 1)
+            quantise_w1(a, 0, 0, first_pair)
             if a == 1:
-                w4_w = place("w4_w", [P, 2 * 2 * H], U8, 18)
-                nc.vector.tensor_copy(
-                    w4_w[:].bitcast(U16).rearrange("p (u t m) -> p u t m", t=PACK, m=P),
-                    w4_raw[:].bitcast(U16).rearrange("p a (g m t) -> p (a g) t m", t=PACK, m=P),
-                )
-            quant_w1(a, 0, 1, bf1)
+                deal_w4(0)
+            quantise_w1(a, 0, 1, second_pair)
             w1_raw[a, 1] = load_w1(a, 1)
+        deal_w4(1)
+        w4_s = place("w4_s", [P, 2, H], U8, W4_S_AT)
+        nc.gpsimd.memset(w4_s[:].bitcast(I32), 0)
+        for a in range(2):
+            move_to_plane(w4_s[:, a, :], w4s_dealt, a)
 
         h = []
-
-        def first_stage(b, i):
-            ht = keep.tile([P, S], F32, name="h%d%d" % (b, i), align_bytes=64)
-            cols = slice(P * (i % 2), P * (i % 2 + 1))
-            for c in range(2):
-                acc = psum.tile([P, BANK], F32, name="acc1", tag="acc1")
-                js = slice(BANK * c, BANK * (c + 1))
-                for a in range(2):
-                    nc.tensor.matmul_mx(
-                        out=acc[:],
-                        lhsT=w1_q[a, b, i // 2][:, cols].bitcast(FP8X4),
-                        lhsT_scale=w1_s[a, b, i // 2][:, cols],
-                        rhs=v_w[a][:, js].bitcast(FP8X4),
-                        rhs_scale=v_s[4 * a : P, js],
-                        start=(a == 0),
-                        stop=(a == 1),
-                    )
-                if (b, i, c) == (0, 0, 1):
-                    nc.vector.tensor_scalar(ht[:, js], acc[:], b1_t[:, b, i : i + 1], 0.0, ALU.add, ALU.max)
-                else:
-                    nc.scalar.activation(ht[:, js], acc[:], ACT.Relu, bias=b1_t[:, b, i : i + 1])
-            h.append(ht)
-
         x_f = {}
         x_q = []
         x_s = []
-        picked = {}
-
-        def pick_first(n):
-            g = ring.tile([P, J], F32, name="picked", tag="picked", align_bytes=64)
-            nc.vector.tensor_copy(g[:], h[n][:].indirect(pos1_t[:]))
-            picked[n] = g
-
-        def pick_second(n):
-            b, i = divmod(n, PACK)
-            if i == 0:
-                x_f[b] = place("x_f%d" % b, [P, PACK, J], F32, 48 + 8 * b)
-            nc.vector.tensor_tensor(x_f[b][:, i, :], h[n][:].indirect(pos2_t[:]), picked[n][:], ALU.add)
-
-        def interleave(engine_copy, dst, src):
-            engine_copy(
-                dst.rearrange("p (c i) t -> p c t i", i=PACK),
-                src.rearrange("p t (c i) -> p c t i", i=PACK),
-            )
-
-        def quant_x(b, engine_copy):
-            bf = ring.tile([P, J, PACK], BF16, name="x_bf", tag="bf4k", bufs=3, align_bytes=64)
-            interleave(engine_copy, bf[:], x_f[b][:])
-            q = keep.tile([P, J], U32, name="x_q%d" % b, align_bytes=64)
-            s = keep.tile([P, J], U8, name="x_s%d" % b, align_bytes=64)
-            nc.vector.quantize_mx(out=q[:].bitcast(FP8X4), scales=s[:], in_=bf[:].rearrange("p c t -> p (c t)"))
-            x_q.append(q)
-            x_s.append(s)
-
-        sh_at = [4, 8, 12, 22, 56, 60, 26, 64]
         sh = {}
 
-        def scale_h(n, engine):
-            st = place("sh%d" % n, [P, S], F32, sh_at[n])
-            factor = skip_t[:, n // PACK, n % PACK : n % PACK + 1]
-            if engine == "scalar":
-                nc.scalar.activation(st[:], h[n][:], ACT.Copy, scale=factor)
-            elif engine == "vector":
-                nc.vector.tensor_scalar(st[:], h[n][:], factor, None, ALU.mult)
+        def first_product(n):
+            b, t = divmod(n, PACK)
+            h_n = keep.tile([P, S], F32, name="h%d%d" % (b, t), align_bytes=64)
+            cols = slice(P * (t % 2), P * (t % 2 + 1))
+            for c in range(S // BANK):
+                acc = psum.tile([P, BANK], F32, name="acc1", tag="acc1")
+                frames = slice(BANK * c, BANK * (c + 1))
+                for a in range(2):
+                    nc.tensor.matmul_mx(
+                        out=acc[:],
+                        lhsT=w1_q[a, b, t // 2][:, cols].bitcast(FP8X4),
+                        lhsT_scale=w1_s[a, b, t // 2][:, cols],
+                        rhs=v_w[a][:, frames].bitcast(FP8X4),
+                        rhs_scale=v_s[a][:, frames],
+                        start=(a == 0),
+                        stop=(a == 1),
+                    )
+                nc.scalar.activation(h_n[:, frames], acc[:], ACT.Relu, bias=b1_t[:, b, t : t + 1])
+            h.append(h_n)
+
+        def pick_pairs(n):
+            b, t = divmod(n, PACK)
+            if n in PICKED_AT:
+                picked = place("picked%d" % n, [P, J], F32, PICKED_AT[n])
             else:
-                nc.gpsimd.tensor_scalar(st[:], h[n][:], factor, 0.0, ALU.mult, ALU.add)
-            sh[n] = st
+                picked = ring.tile([P, J], F32, name="picked", tag="picked", align_bytes=64)
+            for lo in (0, HALF_J):
+                nc.vector.tensor_copy(picked[:, lo : lo + HALF_J], h[n][:].indirect(entries(pos1_t, lo, lo + HALF_J)))
+            if t == 0:
+                x_f[b] = place("x_f%d" % b, [P, PACK, J], F32, X_F_AT[b])
+            for lo in (0, HALF_J):
+                window = h[n][:].indirect(entries(pos2_t, lo, lo + HALF_J))
+                nc.vector.tensor_tensor(x_f[b][:, t, lo : lo + HALF_J], window, picked[:, lo : lo + HALF_J], ALU.add)
 
-        late = {1: [(0, 1, 0)], 2: [(1, 1, 0), (0, 1, 1)], 3: [(1, 1, 1)]}
-        for n in range(8):
-            first_stage(*divmod(n, PACK))
-            pick_first(n)
-            if n > 0:
-                pick_second(n - 1)
-            for a, b, half in late.get(n, []):
-                quant_w1(a, b, half, scalar_cast_w1(a, b, half))
-            if n == 7:
-                quant_x(0, nc.scalar.copy)
-        pick_second(7)
-        quant_x(1, nc.vector.tensor_copy)
-        for n in range(PACK):
-            scale_h(n, "scalar")
+        def interleave(copy, dst, src):
+            copy(dst.rearrange("p (c i) t -> p c t i", i=2), src.rearrange("p t (c i) -> p c t i", i=2))
 
-        def second_pass(acc, g, t, a):
-            u = (2 * a + g) * PACK + t
-            nc.tensor.matmul_mx(
-                out=acc[:],
-                lhsT=w4_w[:, 2 * P * u : 2 * P * (u + 1)].bitcast(FP4X4),
-                lhsT_scale=w4_s[:, P * u : P * (u + 1)],
-                rhs=x_q[a][:].bitcast(FP8X4),
-                rhs_scale=x_s[a][:],
-                start=(a == 0),
-                stop=(a == 1),
-            )
+        def quantise_x(b, copies):
+            rounded = []
+            for u in range(2):
+                half = place("x_bf%d%d" % (b, u), [P, HALF_J, PACK], BF16, X_BF_AT[b] + 2 * u)
+                interleave(copies[u], half[:], x_f[b][:, :, HALF_J * u : HALF_J * (u + 1)])
+                rounded.append(half)
+            codes = place("x_q%d" % b, [P, J], U32, X_Q_AT[b])
+            plane = keep.tile([P, J], U8, name="x_s%d" % b, align_bytes=64)
+            for u in range(2):
+                joints = slice(HALF_J * u, HALF_J * (u + 1))
+                nc.vector.quantize_mx(
+                    out=codes[:, joints].bitcast(FP8X4), scales=plane[:, joints], in_=rounded[u][:].rearrange("p c t -> p (c t)")
+                )
+            x_q.append(codes)
+            x_s.append(plane)
 
-        def second_stage(g):
+        def scale_on_scalar(dst, src, factor):
+            nc.scalar.activation(dst, src, ACT.Copy, scale=factor)
+
+        def scale_on_vector(dst, src, factor):
+            nc.vector.tensor_scalar(dst, src, factor, None, ALU.mult)
+
+        def skip_times_h(n, scale):
+            b, t = divmod(n, PACK)
+            sh[n] = place("sh%d" % n, [P, S], F32, SH_AT[n])
+            scale(sh[n][:], h[n][:], skip_t[:, b, t : t + 1])
+
+        for n in range(SLICES):
+            first_product(n)
+            pick_pairs(n)
+            for a, b, pair in LATE_WEIGHTS.get(n, []):
+                quantise_w1(a, b, pair, round_w1_on_scalar(a, b, pair))
+            if n == 4:
+                skip_times_h(0, scale_on_scalar)
+            if n == 5:
+                quantise_x(0, [nc.scalar.copy, nc.scalar.copy])
+        for n in (1, 2, 7):
+            skip_times_h(n, scale_on_scalar)
+        quantise_x(1, [nc.scalar.copy, nc.vector.tensor_copy])
+        skip_times_h(3, scale_on_scalar)
+
+        def second_product(b):
             accs = [psum.tile([P, BANK], F32, name="acc2", tag="acc2") for t in range(PACK)]
             for a in range(2):
                 for t in range(PACK):
-                    second_pass(accs[t], g, t, a)
+                    word = P * (PACK * a + t)
+                    column = KP * b + P * t
+                    nc.tensor.matmul_mx(
+                        out=accs[t][:],
+                        lhsT=w4_w[b][:, 2 * word : 2 * (word + P)].bitcast(FP4X4),
+                        lhsT_scale=w4_s[:, a, column : column + P],
+                        rhs=x_q[a][:].bitcast(FP8X4),
+                        rhs_scale=x_s[a][:],
+                        start=(a == 0),
+                        stop=(a == 1),
+                    )
             for t in range(PACK):
-                nc.scalar.copy(joint[PACK * g + t][:, 0:J], accs[t][:])
+                nc.scalar.copy(joint[PACK * b + t][:, 0:J], accs[t][:])
 
-        second_stage(0)
-        for n in (4, 5):
-            scale_h(n, "vector")
+        second_product(0)
+        for n in (4, 5, 6):
+            skip_times_h(n, scale_on_vector)
 
-        y_s = [keep.tile([P, S], U8, name="y_s%d" % g, align_bytes=64) for g in range(2)]
+        y_s = [keep.tile([P, S], U8, name="y_s%d" % b, align_bytes=64) for b in range(2)]
 
-        def finish(g, c0, c1, y):
-            w = c1 - c0
-            bf = ring.tile([P, w, PACK], BF16, name="y_bf", tag="bf4k", bufs=3, align_bytes=64)
-            interleave(nc.vector.tensor_copy, bf[:], y[:])
-            q = ring.tile([P, w], U32, name="y_q", tag="y_q", bufs=3, align_bytes=64)
-            nc.vector.quantize_mx(out=q[:].bitcast(FP8X4), scales=y_s[g][:, c0:c1], in_=bf[:].rearrange("p c t -> p (c t)"))
-            nc.sync.dma_start(out_1[g].rearrange("p m t -> p (m t)")[:, PACK * c0 : PACK * c1].bitcast(I32), q[:].bitcast(I32))
-            if c1 == S:
-                for q4 in range(4):
-                    eng = nc.sync if q4 % 2 == 0 or g == 0 else nc.scalar
-                    eng.dma_start(out_2[g, 4 * q4 : 4 * q4 + 4, :].bitcast(I32), y_s[g][32 * q4 : 32 * q4 + 4, :].bitcast(I32))
+        def store_planes(b, first, end, y):
+            width = end - first
+            parts = [(0, 128, nc.vector.tensor_copy), (128, 256, nc.vector.tensor_copy)]
+            if width == BANK:
+                parts.append((256, 512, nc.scalar.copy))
+            rounded = []
+            for lo, hi, copy in parts:
+                part = ring.tile([P, hi - lo, PACK], BF16, name="y_bf", tag="y_bf", bufs=6, align_bytes=64)
+                interleave(copy, part[:], y[:, :, lo:hi])
+                rounded.append(part)
+            codes = ring.tile([P, width], U32, name="y_q", tag="y_q", bufs=3, align_bytes=64)
+            for (lo, hi, copy), part in zip(parts, rounded):
+                nc.vector.quantize_mx(
+                    out=codes[:, lo:hi].bitcast(FP8X4),
+                    scales=y_s[b][:, first + lo : first + hi],
+                    in_=part[:].rearrange("p c t -> p (c t)"),
+                )
+            words_out = out_1[b].rearrange("p m t -> p (m t)")[:, PACK * first : PACK * end]
+            nc.sync.dma_start(words_out.bitcast(I32), codes[:].bitcast(I32))
+            if end == S:
+                for quadrant in range(QUADRANTS):
+                    queue = nc.scalar if b == 1 and quadrant % 2 == 1 else nc.sync
+                    queue.dma_start(
+                        out_2[b, 4 * quadrant : 4 * quadrant + 4, :].bitcast(I32),
+                        y_s[b][32 * quadrant : 32 * quadrant + 4, :].bitcast(I32),
+                    )
 
-        chunks = [(0, 0, 512, 32), (0, 512, 1024, 40), (1, 0, 512, 48), (1, 512, 768, 32), (1, 768, 1024, 36)]
-        waiting = None
-        for k, (g, c0, c1, y_at) in enumerate(chunks):
-            w = c1 - c0
-            last = k == len(chunks) - 1
-            y = place("y%d" % k, [P, PACK, w], F32, y_at)
-            rows = out_0[KP * g : KP * (g + 1), c0:c1].rearrange("(p t) j -> p t j", t=PACK)
+        previous = None
+        for k, (b, first, end, y_at) in enumerate(CHUNKS):
+            width = end - first
+            last = k == len(CHUNKS) - 1
+            y = place("y%d" % k, [P, PACK, width], F32, y_at)
+            rows_out = out_0[KP * b : KP * (b + 1), first:end].rearrange("(p t) j -> p t j", t=PACK)
             for t in range(PACK):
-                n = PACK * g + t
-                z = ring.tile([P, w], F32, name="z", tag="z", bufs=4, align_bytes=64)
-                nc.vector.tensor_tensor(z[:], joint[n][:].indirect(pos3_t[:, c0 // 16 : c1 // 16]), sh[n][:, c0:c1], ALU.add)
-                th = ring.tile([P, w], F32, name="th", tag="th", bufs=2, align_bytes=64)
-                nc.scalar.activation(th[:], z[:], ACT.Tanh)
-                factor = gain_t[:, g, t : t + 1]
-                if last and t == PACK - 1:
-                    nc.vector.tensor_scalar(y[:, t, :], th[:], factor, None, ALU.mult)
-                else:
-                    nc.scalar.activation(y[:, t, :], th[:], ACT.Copy, scale=factor)
-                if t == 1 and waiting is not None:
-                    finish(*waiting)
+                n = PACK * b + t
+                z = ring.tile([P, width], F32, name="z", tag="z", bufs=6, align_bytes=64)
+                nc.vector.tensor_tensor(z[:], joint[n][:].indirect(entries(pos3_t, first, end)), sh[n][:, first:end], ALU.add)
+                squashed = ring.tile([P, width], F32, name="th", tag="th", bufs=2, align_bytes=64)
+                nc.scalar.activation(squashed[:], z[:], ACT.Tanh)
+                scale = scale_on_vector if last and t == PACK - 1 else scale_on_scalar
+                scale(y[:, t, :], squashed[:], gain_t[:, b, t : t + 1])
+                if t == 1 and previous is not None:
+                    store_planes(*previous)
                 if last and t % 2 == 1:
-                    nc.sync.dma_start(rows[:, t - 1 : t + 1, :], y[:, t - 1 : t + 1, :])
+                    nc.sync.dma_start(rows_out[:, t - 1 : t + 1, :], y[:, t - 1 : t + 1, :])
             if not last:
-                nc.sync.dma_start(rows, y[:])
-            waiting = (g, c0, c1, y)
+                nc.sync.dma_start(rows_out, y[:])
+            previous = (b, first, end, y)
             if k == 0:
-                second_stage(1)
-                for n in (6, 7):
-                    scale_h(n, "scalar")
-        finish(*waiting)
+                second_product(1)
+        store_planes(*previous)

from contextlib import ExitStack

import concourse.mybir as mybir

K, T, H, S, J = 1024, 4096, 1024, 1024, 512
FLOPS = 2 * K * H * S + 2 * H * H * J

F32 = mybir.dt.float32
BF16 = mybir.dt.bfloat16
I32 = mybir.dt.int32
U32 = mybir.dt.uint32
U16 = mybir.dt.uint16
U8 = mybir.dt.uint8
FP8X4 = mybir.dt.float8_e4m3fn_x4
FP4X4 = mybir.dt.float4_e2m1fn_x4
ACT = mybir.ActivationFunctionType
ALU = mybir.AluOpType

P = 128
PACK = 4
KP = P * PACK
BANK = 512
SLICES = H // P
QUADRANTS = 4
PER_COLUMN = 16
SPARE = 16
HALF_J = J // 2
KIB = 1024

TAB_W_AT = [0, 16]
W1_RAW_AT = [32, 40]
TAB_S_AT = 40
W4S_ROWS_AT = 47.5
V_S_AT = [49, 48]
W4_RAW_AT = [0, 2]
W1_BF_VECTOR_AT = 16
W1_BF_SCALAR_AT = 68
W4_W_AT = [17, 0]
W4_S_AT = 14.5
W1_Q_LATE_AT = 85.5
PICKED_AT = {3: 78, 4: 80, 5: 82}
X_F_AT = [98, 56]
X_BF_AT = [84, 88]
X_Q_AT = [96, 92]
SH_AT = [40, 44, 32, 36, 60, 88, 56, 64]
CHUNKS = [(0, 0, 512, 4), (0, 512, 1024, 23), (1, 0, 512, 98), (1, 512, 768, 4), (1, 768, 1024, 8)]
LATE_WEIGHTS = {2: [(0, 1, 0), (1, 1, 0)], 3: [(0, 1, 1)], 4: [(1, 1, 1)]}


def tile_list_pipe_joint_encoder_kernel(
    tc, tab_words, tab_scales, offs, pos1, pos2, pos3, w1, b1, w4_words, w4_scales, skip, gain, out_0, out_1, out_2
):
    nc = tc.nc
    with ExitStack() as ctx:
        keep = ctx.enter_context(tc.tile_pool(name="keep", bufs=1))
        arena = ctx.enter_context(tc.tile_pool(name="arena", bufs=1))
        ring = ctx.enter_context(tc.tile_pool(name="ring", bufs=2))
        psum = ctx.enter_context(tc.psum_pool(name="psum", bufs=4))

        def place(name, shape, dtype, kib):
            return arena.tile(shape, dtype, name=name, offset=int(kib * KIB), align_bytes=64)

        def entries(list_tile, first, end):
            return list_tile[:, first // PER_COLUMN : end // PER_COLUMN]

        def load_scale_rows(name, src, kib):
            rows = place(name, [P, src.shape[2] // 4], I32, kib)
            nc.sync.dma_start(rows[0:32, :], src.rearrange("a q c -> (a q) c").bitcast(I32))
            nc.vector.memset(rows[32:64, :], 0)
            nc.vector.memset(rows[64:P, :], 0)
            return rows

        def move_to_plane(plane, rows, a):
            for quadrant in range(QUADRANTS):
                first = 16 * a + 4 * quadrant
                nc.sync.dma_start(plane[32 * quadrant : 32 * quadrant + 4, :].bitcast(I32), rows[first : first + 4, :].bitcast(I32))

        def load_list(name, src):
            list_tile = keep.tile([P, src.shape[1]], U16, name=name)
            nc.sync.dma_start(list_tile[:], src)
            return list_tile

        def load_vector(name, vec):
            values = keep.tile([P, 2, PACK], F32, name=name)
            nc.gpsimd.dma_start(values[:], vec.rearrange("(b p t) -> p b t", b=2, t=PACK))
            return values

        def load_w1(a, b):
            raw = place("w1_raw%d%d" % (a, b), [P, PACK, KP], F32, W1_RAW_AT[a])
            nc.sync.dma_start(raw[:], w1[KP * a : KP * (a + 1), KP * b : KP * (b + 1)].rearrange("(p j) c -> p j c", j=PACK))
            return raw

        def load_table(a):
            words = place("tab_w%d" % a, [P, T], U32, TAB_W_AT[a])
            nc.sync.dma_start(words[:].bitcast(I32), tab_words[a].rearrange("p t i -> p (t i)").bitcast(I32))
            return words

        def load_w4(b):
            raw = place("w4_raw%d" % b, [P, 2, 2 * KP], U8, W4_RAW_AT[b])
            src = w4_words.rearrange("a p c -> p a c")[:, :, 2 * KP * b : 2 * KP * (b + 1)]
            nc.sync.dma_start(raw[:].bitcast(I32), src.bitcast(I32))
            return raw

        offs_t = load_list("offs_t", offs)
        tab_s = load_scale_rows("tab_s", tab_scales, TAB_S_AT)
        w4s_rows = load_scale_rows("w4s_rows", w4_scales, W4S_ROWS_AT)
        tab_w = [load_table(0)]
        pos1_t = load_list("pos1_t", pos1)
        pos2_t = load_list("pos2_t", pos2)
        pos3_t = load_list("pos3_t", pos3)
        tab_w.append(load_table(1))
        w1_raw = {(0, 0): load_w1(0, 0)}

        vs_rows = keep.tile([P, S], U8, name="vs_rows", align_bytes=64)
        nc.vector.tensor_copy(vs_rows[:], tab_s[:].bitcast(U8).indirect(offs_t[:]))
        w4s_dealt = keep.tile([P, H], U8, name="w4s_dealt", align_bytes=64)
        nc.vector.tensor_copy(
            w4s_dealt[:].rearrange("p (b t m) -> p b t m", t=PACK, m=P),
            w4s_rows[:].bitcast(U8).rearrange("p (b m t) -> p b t m", t=PACK, m=P),
        )

        def table_plane(a):
            plane = place("v_s%d" % a, [P, S], U8, V_S_AT[a])
            nc.gpsimd.memset(plane[:].bitcast(I32), 0)
            move_to_plane(plane, vs_rows, a)
            return plane

        v_s = [table_plane(0)]
        b1_t = load_vector("b1_t", b1)
        skip_t = load_vector("skip_t", skip)
        gain_t = load_vector("gain_t", gain)
        w1_raw[1, 0] = load_w1(1, 0)
        v_s.append(table_plane(1))

        joint = []
        for n in range(SLICES):
            joint_n = keep.tile([P, J + SPARE], F32, name="joint%d" % n, align_bytes=64)
            nc.gpsimd.memset(joint_n[:, J:], 0.0)
            joint.append(joint_n)

        v_w = []
        for a in range(2):
            words = keep.tile([P, S], U32, name="v_w%d" % a, align_bytes=64)
            nc.vector.tensor_copy(words[:], tab_w[a][:].indirect(offs_t[:]))
            v_w.append(words)
            if a == 0:
                w4_raw = [load_w4(0), load_w4(1)]

        w1_q = {}
        w1_s = {}
        w4_w = {}

        def round_w1(a, b, pair, copy, rounded):
            src = w1_raw[a, b][:].rearrange("p j (m t) -> p m j t", t=PACK)[:, :, :, 2 * pair : 2 * pair + 2]
            copy(rounded[:].rearrange("p t m j -> p m j t"), src)
            return rounded

        def round_w1_on_scalar(a, b, pair):
            kib = W1_BF_SCALAR_AT + 2 * (4 * b + 2 * pair + a)
            return round_w1(a, b, pair, nc.scalar.copy, place("w1_bf%d%d%d" % (a, b, pair), [P, 2, P, PACK], BF16, kib))

        def quantise_w1(a, b, pair, rounded):
            if (a, b, pair) == (1, 1, 0):
                codes = place("w1_q110", [P, 2 * P], U32, W1_Q_LATE_AT)
            else:
                codes = keep.tile([P, 2 * P], U32, name="w1_q%d%d%d" % (a, b, pair), align_bytes=64)
            plane = keep.tile([P, 2 * P], U8, name="w1_s%d%d%d" % (a, b, pair), align_bytes=64)
            nc.vector.quantize_mx(out=codes[:].bitcast(FP8X4), scales=plane[:], in_=rounded[:].rearrange("p t m j -> p (t m j)"))
            w1_q[a, b, pair] = codes
            w1_s[a, b, pair] = plane

        def deal_w4(b):
            w4_w[b] = place("w4_w%d" % b, [P, 2 * 2 * KP], U8, W4_W_AT[b])
            nc.vector.tensor_copy(
                w4_w[b][:].bitcast(U16).rearrange("p (a t m) -> p a t m", t=PACK, m=P),
                w4_raw[b][:].bitcast(U16).rearrange("p a (m t) -> p a t m", t=PACK),
            )

        for a in range(2):
            first_pair = round_w1(a, 0, 0, nc.vector.tensor_copy, place("w1_bfv%d" % a, [P, 2, P, PACK], BF16, W1_BF_VECTOR_AT))
            second_pair = round_w1_on_scalar(a, 0, 1)
            quantise_w1(a, 0, 0, first_pair)
            if a == 1:
                deal_w4(0)
            quantise_w1(a, 0, 1, second_pair)
            w1_raw[a, 1] = load_w1(a, 1)
        deal_w4(1)
        w4_s = place("w4_s", [P, 2, H], U8, W4_S_AT)
        nc.gpsimd.memset(w4_s[:].bitcast(I32), 0)
        for a in range(2):
            move_to_plane(w4_s[:, a, :], w4s_dealt, a)

        h = []
        x_f = {}
        x_q = []
        x_s = []
        sh = {}

        def first_product(n):
            b, t = divmod(n, PACK)
            h_n = keep.tile([P, S], F32, name="h%d%d" % (b, t), align_bytes=64)
            cols = slice(P * (t % 2), P * (t % 2 + 1))
            for c in range(S // BANK):
                acc = psum.tile([P, BANK], F32, name="acc1", tag="acc1")
                frames = slice(BANK * c, BANK * (c + 1))
                for a in range(2):
                    nc.tensor.matmul_mx(
                        out=acc[:],
                        lhsT=w1_q[a, b, t // 2][:, cols].bitcast(FP8X4),
                        lhsT_scale=w1_s[a, b, t // 2][:, cols],
                        rhs=v_w[a][:, frames].bitcast(FP8X4),
                        rhs_scale=v_s[a][:, frames],
                        start=(a == 0),
                        stop=(a == 1),
                    )
                nc.scalar.activation(h_n[:, frames], acc[:], ACT.Relu, bias=b1_t[:, b, t : t + 1])
            h.append(h_n)

        def pick_pairs(n):
            b, t = divmod(n, PACK)
            if n in PICKED_AT:
                picked = place("picked%d" % n, [P, J], F32, PICKED_AT[n])
            else:
                picked = ring.tile([P, J], F32, name="picked", tag="picked", align_bytes=64)
            for lo in (0, HALF_J):
                nc.vector.tensor_copy(picked[:, lo : lo + HALF_J], h[n][:].indirect(entries(pos1_t, lo, lo + HALF_J)))
            if t == 0:
                x_f[b] = place("x_f%d" % b, [P, PACK, J], F32, X_F_AT[b])
            for lo in (0, HALF_J):
                window = h[n][:].indirect(entries(pos2_t, lo, lo + HALF_J))
                nc.vector.tensor_tensor(x_f[b][:, t, lo : lo + HALF_J], window, picked[:, lo : lo + HALF_J], ALU.add)

        def interleave(copy, dst, src):
            copy(dst.rearrange("p (c i) t -> p c t i", i=2), src.rearrange("p t (c i) -> p c t i", i=2))

        def quantise_x(b, copies):
            rounded = []
            for u in range(2):
                half = place("x_bf%d%d" % (b, u), [P, HALF_J, PACK], BF16, X_BF_AT[b] + 2 * u)
                interleave(copies[u], half[:], x_f[b][:, :, HALF_J * u : HALF_J * (u + 1)])
                rounded.append(half)
            codes = place("x_q%d" % b, [P, J], U32, X_Q_AT[b])
            plane = keep.tile([P, J], U8, name="x_s%d" % b, align_bytes=64)
            for u in range(2):
                joints = slice(HALF_J * u, HALF_J * (u + 1))
                nc.vector.quantize_mx(
                    out=codes[:, joints].bitcast(FP8X4), scales=plane[:, joints], in_=rounded[u][:].rearrange("p c t -> p (c t)")
                )
            x_q.append(codes)
            x_s.append(plane)

        def scale_on_scalar(dst, src, factor):
            nc.scalar.activation(dst, src, ACT.Copy, scale=factor)

        def scale_on_vector(dst, src, factor):
            nc.vector.tensor_scalar(dst, src, factor, None, ALU.mult)

        def skip_times_h(n, scale):
            b, t = divmod(n, PACK)
            sh[n] = place("sh%d" % n, [P, S], F32, SH_AT[n])
            scale(sh[n][:], h[n][:], skip_t[:, b, t : t + 1])

        for n in range(SLICES):
            first_product(n)
            pick_pairs(n)
            for a, b, pair in LATE_WEIGHTS.get(n, []):
                quantise_w1(a, b, pair, round_w1_on_scalar(a, b, pair))
            if n == 4:
                skip_times_h(0, scale_on_scalar)
            if n == 5:
                quantise_x(0, [nc.scalar.copy, nc.scalar.copy])
        for n in (1, 2, 7):
            skip_times_h(n, scale_on_scalar)
        quantise_x(1, [nc.scalar.copy, nc.vector.tensor_copy])
        skip_times_h(3, scale_on_scalar)

        def second_product(b):
            accs = [psum.tile([P, BANK], F32, name="acc2", tag="acc2") for t in range(PACK)]
            for a in range(2):
                for t in range(PACK):
                    word = P * (PACK * a + t)
                    column = KP * b + P * t
                    nc.tensor.matmul_mx(
                        out=accs[t][:],
                        lhsT=w4_w[b][:, 2 * word : 2 * (word + P)].bitcast(FP4X4),
                        lhsT_scale=w4_s[:, a, column : column + P],
                        rhs=x_q[a][:].bitcast(FP8X4),
                        rhs_scale=x_s[a][:],
                        start=(a == 0),
                        stop=(a == 1),
                    )
            for t in range(PACK):
                nc.scalar.copy(joint[PACK * b + t][:, 0:J], accs[t][:])

        second_product(0)
        for n in (4, 5, 6):
            skip_times_h(n, scale_on_vector)

        y_s = [keep.tile([P, S], U8, name="y_s%d" % b, align_bytes=64) for b in range(2)]

        def store_planes(b, first, end, y):
            width = end - first
            parts = [(0, 128, nc.vector.tensor_copy), (128, 256, nc.vector.tensor_copy)]
            if width == BANK:
                parts.append((256, 512, nc.scalar.copy))
            rounded = []
            for lo, hi, copy in parts:
                part = ring.tile([P, hi - lo, PACK], BF16, name="y_bf", tag="y_bf", bufs=6, align_bytes=64)
                interleave(copy, part[:], y[:, :, lo:hi])
                rounded.append(part)
            codes = ring.tile([P, width], U32, name="y_q", tag="y_q", bufs=3, align_bytes=64)
            for (lo, hi, copy), part in zip(parts, rounded):
                nc.vector.quantize_mx(
                    out=codes[:, lo:hi].bitcast(FP8X4),
                    scales=y_s[b][:, first + lo : first + hi],
                    in_=part[:].rearrange("p c t -> p (c t)"),
                )
            words_out = out_1[b].rearrange("p m t -> p (m t)")[:, PACK * first : PACK * end]
            nc.sync.dma_start(words_out.bitcast(I32), codes[:].bitcast(I32))
            if end == S:
                for quadrant in range(QUADRANTS):
                    queue = nc.scalar if b == 1 and quadrant % 2 == 1 else nc.sync
                    queue.dma_start(
                        out_2[b, 4 * quadrant : 4 * quadrant + 4, :].bitcast(I32),
                        y_s[b][32 * quadrant : 32 * quadrant + 4, :].bitcast(I32),
                    )

        previous = None
        for k, (b, first, end, y_at) in enumerate(CHUNKS):
            width = end - first
            last = k == len(CHUNKS) - 1
            y = place("y%d" % k, [P, PACK, width], F32, y_at)
            rows_out = out_0[KP * b : KP * (b + 1), first:end].rearrange("(p t) j -> p t j", t=PACK)
            for t in range(PACK):
                n = PACK * b + t
                z = ring.tile([P, width], F32, name="z", tag="z", bufs=6, align_bytes=64)
                nc.vector.tensor_tensor(z[:], joint[n][:].indirect(entries(pos3_t, first, end)), sh[n][:, first:end], ALU.add)
                squashed = ring.tile([P, width], F32, name="th", tag="th", bufs=2, align_bytes=64)
                nc.scalar.activation(squashed[:], z[:], ACT.Tanh)
                scale = scale_on_vector if last and t == PACK - 1 else scale_on_scalar
                scale(y[:, t, :], squashed[:], gain_t[:, b, t : t + 1])
                if t == 1 and previous is not None:
                    store_planes(*previous)
                if last and t % 2 == 1:
                    nc.sync.dma_start(rows_out[:, t - 1 : t + 1, :], y[:, t - 1 : t + 1, :])
            if not last:
                nc.sync.dma_start(rows_out, y[:])
            previous = (b, first, end, y)
            if k == 0:
                second_product(1)
        store_planes(*previous)
